import numpy as np
import ml_dtypes


def mxq(x, axis, fmt="e4m3"):
    dtype, down = {"e4m3": (ml_dtypes.float8_e4m3fn, 7), "e5m2": (ml_dtypes.float8_e5m2, 14)}[fmt]
    v = np.moveaxis(np.asarray(x, np.float32).astype(ml_dtypes.bfloat16).astype(np.float64), axis, -1)
    blocks = v.reshape(v.shape[:-1] + (-1, 32))
    amax = np.abs(blocks).max(-1, keepdims=True)
    byte = np.maximum(np.where(amax > 0, np.frexp(amax)[1] - 1 + 127, 0) - down, 1)
    scale = np.exp2(byte - 127.0)
    codes = (blocks / scale).astype(np.float32).astype(dtype).astype(np.float64)
    return np.moveaxis((codes * scale).reshape(v.shape), -1, axis)


WIDE = False


def mx_kscale(k):
    if not WIDE:
        return np.ones(k)
    levels = np.array([10, -10, 5, -5, 0])
    if k % 512:
        return np.exp2(np.random.permutation(np.resize(levels, k // 32))).repeat(32)
    a = np.empty((k // 512, 16))
    for p in range(k // 512):
        a[p, :8] = np.random.permutation(np.resize(levels, 8))
        for g in range(8):
            far = levels[np.abs(levels - a[p, g]) >= 10]
            a[p, g + 8] = far[np.random.randint(len(far))]
    return np.exp2(a.ravel()).repeat(32)


BF16 = ml_dtypes.bfloat16


def bf(x):
    return np.asarray(x, np.float32).astype(BF16)


def f64(x):
    return np.asarray(x).astype(np.float64)

def planes(Y):
    n, m = Y.shape
    b = f64(bf(Y)).reshape(n // 32, 32, m)
    amax = np.abs(b).max(1)
    byte = np.clip(np.where(amax > 0, np.frexp(amax)[1] - 1 + 127 - 7, 1), 1, 254)
    codes = (b * np.exp2(127.0 - byte)[:, None, :]).reshape(n, m).astype(np.float32).astype(ml_dtypes.float8_e4m3fn).view(np.uint8)
    words = codes.reshape(n // 512, 128, 4, m).transpose(0, 1, 3, 2)
    return np.ascontiguousarray(words), np.ascontiguousarray(byte.astype(np.uint8).reshape(n // 512, 16, m))


B, T, F, D, S = 4, 1024, 512, 1024, 384

def setup_inputs():
    s = mx_kscale(F)
    t = mx_kscale(T)
    mel = np.random.randn(B, T, F) * s
    w_in = np.random.randn(F, D) / np.sqrt(F) / s[:, None]
    frame_gain = np.exp(0.4 * np.random.randn(B, T)) * t
    w_bottle = np.random.randn(T, S) / np.sqrt(T) / t[:, None]
    offset = 0.5 * np.random.randn(B, D)
    gamma = np.exp(0.8 * np.random.randn(D))
    return {"mel": bf(mel), "w_in": bf(w_in), "frame_gain": bf(frame_gain),
            "w_bottle": bf(w_bottle), "offset": bf(offset), "gamma": bf(gamma)}

def reference(mel, w_in, frame_gain, w_bottle, offset, gamma):
    x, w, v = f64(mel), f64(w_in), f64(w_bottle)
    a = mxq(x, 2) @ mxq(w, 0)
    h = np.maximum(a, 0.0) * f64(frame_gain)[:, :, None]
    z = mxq(v, 0).T @ mxq(h, 1)
    y = np.tanh(z + f64(offset)[:, None, :]) * f64(gamma)
    Y = y.reshape(B * S, D).T
    words, scales = planes(Y)
    return y, words, scales

@@ -1,0 +1,374 @@
+from contextlib import ExitStack
+
+import concourse.mybir as mybir
+from concourse.masks import make_identity
+
+B, T, F, D, S = 4, 1024, 512, 1024, 384
+FLOPS = 2 * B * T * F * D + 2 * B * S * T * D
+
+F32 = mybir.dt.float32
+BF16 = mybir.dt.bfloat16
+I32 = mybir.dt.int32
+U32 = mybir.dt.uint32
+U8 = mybir.dt.uint8
+FP8X4 = mybir.dt.float8_e4m3fn_x4
+ACT = mybir.ActivationFunctionType
+ALU = mybir.AluOpType
+
+P = 128
+PACK = 4
+KP = P * PACK
+STEPS = B * 2 * PACK
+WIDE = 256
+GAMMA_ENG = "S"
+CAST_A = "V"
+CAST_B = "S"
+
+
+def tile_mel_temporal_bottleneck_h3_kernel(
+    tc, mel, w_in, frame_gain, w_bottle, offset, gamma, out_0, out_1, out_2
+):
+    nc = tc.nc
+    with ExitStack() as ctx:
+        keep = ctx.enter_context(tc.tile_pool(name="keep", bufs=1))
+        work = ctx.enter_context(tc.tile_pool(name="work", bufs=3))
+        psum = ctx.enter_context(tc.psum_pool(name="psum", bufs=4))
+        ctx.enter_context(tc.manual_schedule())
+
+        ident = keep.tile([P, P], F32)
+        make_identity(nc, ident[:])
+
+        mel_raw = {}
+
+        def load_mel(b, fg, halves):
+            rows = mel[b, fg * KP : (fg + 1) * KP, :].rearrange("(m t) k -> m t k", t=PACK)
+            n = PACK // halves
+            for h in range(halves):
+                raw = keep.tile([P, n, F], BF16, name="mel_%d_%d_%d" % (b, fg, h))
+                nc.sync.dma_start(out=raw[:], in_=rows[:, h * n : (h + 1) * n, :])
+                for t in range(n):
+                    mel_raw[b, fg, h * n + t] = raw[:, t, :]
+
+        w_raw = {}
+
+        def load_w(gd):
+            raw = keep.tile([P, PACK, KP], BF16, name="w_raw_%d" % gd)
+            nc.sync.dma_start(
+                out=raw[:],
+                in_=w_in[:, gd * KP : (gd + 1) * KP].rearrange("(p j) c -> p j c", j=PACK),
+            )
+            w_raw[gd] = raw
+
+        load_mel(0, 0, 2)
+        load_w(0)
+        gamma_bf = keep.tile([P, 2, PACK], BF16)
+        nc.scalar.dma_start(out=gamma_bf[:], in_=gamma.rearrange("(g p t) -> p g t", p=P, t=PACK))
+        gain = keep.tile([P, B * 2, PACK], BF16)
+        nc.scalar.dma_start(
+            out=gain[:], in_=frame_gain.rearrange("b (g p t) -> p (b g) t", p=P, t=PACK)
+        )
+        shift = keep.tile([P, B * 2, PACK], BF16)
+        nc.scalar.dma_start(
+            out=shift[:], in_=offset.rearrange("b (g p t) -> p (b g) t", p=P, t=PACK)
+        )
+        load_mel(0, 1, 1)
+        v_raw = keep.tile([P, 2, PACK, S], BF16)
+        nc.sync.dma_start(
+            out=v_raw[:], in_=w_bottle.rearrange("(g p j) s -> p g j s", p=P, j=PACK)
+        )
+        load_w(1)
+        for b in range(1, B):
+            for fg in range(2):
+                load_mel(b, fg, 1)
+
+        gamma_f = keep.tile([P, 2, PACK], F32)
+        nc.scalar.activation(out=gamma_f[:], in_=gamma_bf[:], func=ACT.Copy)
+
+        def quantize(codes, scales, src):
+            nc.vector.quantize_mx(out=codes.bitcast(FP8X4), scales=scales, in_=src)
+
+        def copy_on(eng, out, in_):
+            if eng == "V":
+                nc.vector.tensor_copy(out=out, in_=in_)
+            elif eng == "S":
+                nc.scalar.copy(out=out, in_=in_)
+            else:
+                nc.gpsimd.tensor_scalar(
+                    out=out, in0=in_, scalar1=1.0, scalar2=-0.0, op0=ALU.mult, op1=ALU.add
+                )
+
+        w_codes = keep.tile([P, D], U32, align_bytes=64)
+        w_scales = keep.tile([P, D], U8, align_bytes=64)
+        w_grouped = {}
+
+        def w_group(gd, eng):
+            g = keep.tile([P, KP * PACK], BF16, name="w_grouped_%d" % gd, align_bytes=64)
+            copy_on(
+                eng,
+                g[:].rearrange("p (t m j) -> p m j t", t=PACK, j=PACK),
+                w_raw[gd][:].rearrange("p j (m t) -> p m j t", t=PACK),
+            )
+            w_grouped[gd] = g
+
+        def w_quant(gd):
+            cols = slice(gd * KP, (gd + 1) * KP)
+            quantize(w_codes[:, cols], w_scales[:, cols], w_grouped[gd][:])
+
+        v_grouped = keep.tile([P, 2 * S * PACK], BF16, align_bytes=64)
+        v_codes = keep.tile([P, 2 * S], U32, align_bytes=64)
+        v_scales = keep.tile([P, 2 * S], U8, align_bytes=64)
+
+        def v_group(g, eng):
+            copy_on(
+                eng,
+                v_grouped[:, g * S * PACK : (g + 1) * S * PACK].rearrange(
+                    "p (c i j) -> p c j i", i=4, j=PACK
+                ),
+                v_raw[:, g, :, :].rearrange("p j (c i) -> p c j i", i=4),
+            )
+
+        def v_quant():
+            for lo, hi in ((0, 512), (512, 768)):
+                quantize(v_codes[:, lo:hi], v_scales[:, lo:hi], v_grouped[:, lo * PACK : hi * PACK])
+
+        x_grouped = {}
+        x_quant = {}
+
+        def mel_turn(b, fg):
+            for h in range(2):
+                bank = psum.tile([P, 512], F32, tag="sbank", name="mel_bank")
+                for tt in range(2):
+                    words = mel_raw[b, fg, 2 * h + tt].bitcast(F32)
+                    for u in range(2):
+                        c = (2 * tt + u) * P
+                        nc.tensor.transpose(bank[:, c : c + P], words[:, u : 2 * P : 2], ident[:])
+                xg = work.tile([P, 2 * P * PACK], BF16, tag="xg", bufs=4, align_bytes=64)
+                nc.scalar.copy(
+                    out=xg[:].bitcast(F32).rearrange("p (t m u) -> p t m u", t=2, u=2),
+                    in_=bank[:].rearrange("p (t u m) -> p t m u", t=2, u=2),
+                )
+                x_grouped[b, fg, h] = xg
+
+        def mel_quant(b, fg):
+            codes = work.tile([P, KP], U32, tag="xq", bufs=4, align_bytes=64)
+            scales = work.tile([P, KP], U8, tag="xs", bufs=4, align_bytes=64)
+            for h in range(2):
+                cols = slice(h * 2 * P, (h + 1) * 2 * P)
+                quantize(codes[:, cols], scales[:, cols], x_grouped[b, fg, h][:])
+            x_quant[b, fg] = (codes, scales)
+
+        a_banks = {}
+        h_bf = {}
+        h_quant = {}
+
+        def stage1(s):
+            b = s // 8
+            cols = slice((s % 8) * P, (s % 8 + 1) * P)
+            for fg in range(2):
+                codes, scales = x_quant[b, fg]
+                bank = psum.tile([P, 512], F32, tag="abank", name="a_bank")
+                for t in range(PACK):
+                    fr = slice(t * P, (t + 1) * P)
+                    nc.tensor.matmul_mx(
+                        out=bank[:, fr],
+                        lhsT=codes[:, fr].bitcast(FP8X4),
+                        lhsT_scale=scales[:, fr],
+                        rhs=w_codes[:, cols].bitcast(FP8X4),
+                        rhs_scale=w_scales[:, cols],
+                        start=True,
+                        stop=True,
+                    )
+                a_banks[s, fg] = bank
+
+        def relu_gain(s):
+            b = s // 8
+            hb = work.tile([P, 2, P, PACK], BF16, tag="hb", align_bytes=64)
+            for fg in range(2):
+                nc.vector.scalar_tensor_tensor(
+                    out=hb[:, fg, :, :],
+                    in0=a_banks[s, fg][:].rearrange("p (t n) -> p n t", t=PACK),
+                    scalar=0.0,
+                    in1=gain[:, 2 * b + fg, :].unsqueeze(1).to_broadcast([P, P, PACK]),
+                    op0=ALU.max,
+                    op1=ALU.mult,
+                )
+            h_bf[s] = hb
+
+        def h_quantize(s):
+            codes = work.tile([P, 2 * P], U32, tag="hq", align_bytes=64)
+            scales = work.tile([P, 2 * P], U8, tag="hs", align_bytes=64)
+            quantize(codes[:], scales[:], h_bf[s][:].rearrange("p g n t -> p (g n t)"))
+            h_quant[s] = (codes, scales)
+
+        tanh_out = {}
+        y_t = {}
+
+        def stage2(s):
+            codes, scales = h_quant[s]
+            bank = psum.tile([P, 512], F32, tag="sbank", name="z_bank")
+            for lo, hi in ((0, WIDE), (WIDE, S)):
+                for fg in range(2):
+                    ch = slice(fg * P, (fg + 1) * P)
+                    sl = slice(fg * S + lo, fg * S + hi)
+                    nc.tensor.matmul_mx(
+                        out=bank[:, lo:hi],
+                        lhsT=codes[:, ch].bitcast(FP8X4),
+                        lhsT_scale=scales[:, ch],
+                        rhs=v_codes[:, sl].bitcast(FP8X4),
+                        rhs_scale=v_scales[:, sl],
+                        start=(fg == 0),
+                        stop=(fg == 1),
+                    )
+            th = work.tile([P, S], F32, tag="th")
+            nc.scalar.activation(
+                out=th[:],
+                in_=bank[:, 0:S],
+                func=ACT.Tanh,
+                bias=shift[:, s // PACK, s % PACK : s % PACK + 1],
+            )
+            tanh_out[s] = th
+
+        def feature_gain(s, eng):
+            u, t = divmod(s, PACK)
+            if t == 0:
+                y_t[u] = work.tile([P, PACK, S], F32, tag="yt", name="y_t")
+            col = gamma_f[:, u % 2, t : t + 1]
+            if eng == "S":
+                nc.scalar.activation(out=y_t[u][:, t, :], in_=tanh_out[s][:], func=ACT.Copy, scale=col)
+            elif eng == "V":
+                nc.vector.tensor_scalar(
+                    out=y_t[u][:, t, :], in0=tanh_out[s][:], scalar1=col, scalar2=None, op0=ALU.mult
+                )
+            else:
+                nc.gpsimd.tensor_scalar(
+                    out=y_t[u][:, t, :], in0=tanh_out[s][:], scalar1=col, scalar2=-0.0,
+                    op0=ALU.mult, op1=ALU.add,
+                )
+
+        def y_transpose(u, t, j, bank):
+            nc.tensor.transpose(
+                bank[:, t * P : (t + 1) * P], y_t[u][:, t, j * P : (j + 1) * P], ident[:]
+            )
+
+        def y_rows(u):
+            b, gd = divmod(u, 2)
+            return out_0[b, :, gd * KP : (gd + 1) * KP].rearrange("(j s) d -> s j d", s=P)
+
+        def y_evacuate(bank, dst):
+            nc.scalar.copy(
+                out=dst.rearrange("s (p t) -> s p t", t=PACK),
+                in_=bank[:].rearrange("s (t p) -> s p t", t=PACK),
+            )
+
+        def y_store(u):
+            rows = work.tile([P, 3, KP], F32, tag="yrows", bufs=2)
+            for j in range(3):
+                bank = psum.tile([P, 512], F32, tag="sbank", name="y_bank")
+                for t in range(PACK):
+                    y_transpose(u, t, j, bank)
+                y_evacuate(bank, rows[:, j, :])
+            nc.sync.dma_start(out=y_rows(u), in_=rows[:])
+
+        y_bf = {}
+        PARTS = ((0, WIDE), (WIDE, S))
+
+        def y_round(u, part, eng):
+            lo, hi = PARTS[part]
+            yb = work.tile([P, (hi - lo) * PACK], BF16, tag="yb%d" % part, name="y_bf", bufs=2, align_bytes=64)
+            n = 1 if eng != "G" else (hi - lo) // 128
+            w = (hi - lo) // n
+            for c in range(n):
+                copy_on(
+                    eng,
+                    yb[:, c * w * PACK : (c + 1) * w * PACK].rearrange("p (c i t) -> p c t i", i=4, t=PACK),
+                    y_t[u][:, :, lo + c * w : lo + (c + 1) * w].rearrange("p t (c i) -> p c t i", i=4),
+                )
+            y_bf[u, part] = yb
+
+        y_scales = keep.tile([P, B * S], U8, align_bytes=64)
+
+        def y_quant(u):
+            b, gd = divmod(u, 2)
+            codes = work.tile([P, S], U32, tag="yq", bufs=2, align_bytes=64)
+            for part in range(2):
+                lo, hi = PARTS[part]
+                quantize(
+                    codes[:, lo:hi],
+                    y_scales[4 * gd : P, b * S + lo : b * S + hi],
+                    y_bf[u, part][:],
+                )
+            dst = out_1[gd].rearrange("p m t -> p (m t)").bitcast(I32)
+            nc.sync.dma_start(out=dst[:, b * S : (b + 1) * S], in_=codes[:].bitcast(I32))
+
+        mel_turn(0, 0)
+        w_group(0, "V")
+        w_quant(0)
+        mel_quant(0, 0)
+        mel_turn(0, 1)
+        v_group(0, "V")
+        mel_quant(0, 1)
+        v_group(1, "S")
+        w_group(1, "S")
+        stage1(0)
+
+        for i in range(STEPS):
+            t = i % PACK
+            if i + 1 < STEPS:
+                stage1(i + 1)
+            if i >= 2:
+                stage2(i - 2)
+            if i >= 3:
+                feature_gain(i - 3, GAMMA_ENG)
+            nxt = (i // 8 + 1, (i // 4) % 2)
+            if t == 1 and nxt[0] < B:
+                mel_turn(nxt[0], nxt[1])
+            if t == 3 and i >= 7:
+                y_store(i // PACK - 1)
+            if t == 0 and i >= 8:
+                y_round(i // PACK - 2, 1, CAST_B)
+            relu_gain(i)
+            if i >= 1:
+                h_quantize(i - 1)
+            if i == 0:
+                v_quant()
+            if i == 2:
+                w_quant(1)
+            if t == 2 and nxt[0] < B:
+                mel_quant(nxt[0], nxt[1])
+            if t == 3 and 7 <= i < STEPS - 1:
+                y_round(i // PACK - 1, 0, CAST_A)
+            if t == 1 and i >= 9:
+                y_quant(i // PACK - 2)
+
+        last = STEPS // PACK - 1
+        h_quantize(STEPS - 1)
+        feature_gain(STEPS - 3, "S")
+        stage2(STEPS - 2)
+        stage2(STEPS - 1)
+        y_round(last - 1, 0, "V")
+        y_round(last - 1, 1, "V")
+        feature_gain(STEPS - 2, "V")
+        feature_gain(STEPS - 1, "V")
+        banks = []
+        for j in range(3):
+            bank = psum.tile([P, 512], F32, tag="abank", name="last_bank")
+            banks.append(bank)
+        for t in range(PACK):
+            for j in range(3):
+                y_transpose(last, t, j, banks[j])
+        y_quant(last - 1)
+        y_round(last, 0, "V")
+        y_round(last, 1, "V")
+        for j in range(2):
+            rows = keep.tile([P, KP], F32, name="last_rows_%d" % j)
+            y_evacuate(banks[j], rows[:])
+            nc.sync.dma_start(out=y_rows(last)[:, j, :], in_=rows[:])
+        rows = keep.tile([P, KP], F32, name="last_rows_2")
+        y_evacuate(banks[2], rows[:])
+        nc.scalar.dma_start(out=y_rows(last)[:, 2, :], in_=rows[:])
+        y_quant(last)
+        for q in range(4):
+            nc.sync.dma_start(
+                out=out_2[:, 4 * q : 4 * q + 4, :].bitcast(I32),
+                in_=y_scales[32 * q : 32 * q + 8, :].bitcast(I32),
+            )

@@ -17,12 +17,14 @@ ALU = mybir.AluOpType
 
 P = 128
 PACK = 4
-KP = P * PACK
-STEPS = B * 2 * PACK
-WIDE = 256
-GAMMA_ENG = "S"
-CAST_A = "V"
-CAST_B = "S"
+GROUP = P * PACK
+GROUPS = 2
+UNITS = B * GROUPS
+STEPS = UNITS * PACK
+SLOT_TILES = S // P
+RUN = 4
+WIDE = (0, 256)
+NARROW = (256, S)
 
 
 def tile_mel_temporal_bottleneck_h3_kernel(
@@ -31,7 +33,7 @@ def tile_mel_temporal_bottleneck_h3_kernel(
     nc = tc.nc
     with ExitStack() as ctx:
         keep = ctx.enter_context(tc.tile_pool(name="keep", bufs=1))
-        work = ctx.enter_context(tc.tile_pool(name="work", bufs=3))
+        work = ctx.enter_context(tc.tile_pool(name="work", bufs=4))
         psum = ctx.enter_context(tc.psum_pool(name="psum", bufs=4))
         ctx.enter_context(tc.manual_schedule())
 
@@ -39,211 +41,210 @@ def tile_mel_temporal_bottleneck_h3_kernel(
         make_identity(nc, ident[:])
 
         mel_raw = {}
-
-        def load_mel(b, fg, halves):
-            rows = mel[b, fg * KP : (fg + 1) * KP, :].rearrange("(m t) k -> m t k", t=PACK)
-            n = PACK // halves
-            for h in range(halves):
-                raw = keep.tile([P, n, F], BF16, name="mel_%d_%d_%d" % (b, fg, h))
-                nc.sync.dma_start(out=raw[:], in_=rows[:, h * n : (h + 1) * n, :])
-                for t in range(n):
-                    mel_raw[b, fg, h * n + t] = raw[:, t, :]
-
         w_raw = {}
+        gains = {}
 
-        def load_w(gd):
-            raw = keep.tile([P, PACK, KP], BF16, name="w_raw_%d" % gd)
+        def load_mel(n, lo, hi):
+            first = (n % GROUPS) * GROUP
+            rows = mel[n // GROUPS, first : first + GROUP, :].rearrange("(m t) k -> m t k", t=PACK)
+            raw = keep.tile([P, hi - lo, F], BF16, name="mel_%d_%d" % (n, lo))
+            nc.sync.dma_start(out=raw[:], in_=rows[:, lo:hi, :])
+            for t in range(lo, hi):
+                mel_raw[n, t] = raw[:, t - lo, :]
+
+        def load_w(g, half):
+            raw = keep.tile([P, PACK, GROUP // 2], BF16, name="w_raw_%d_%d" % (g, half))
+            lo = g * GROUP + half * GROUP // 2
+            nc.sync.dma_start(
+                out=raw[:], in_=w_in[:, lo : lo + GROUP // 2].rearrange("(p j) c -> p j c", j=PACK)
+            )
+            w_raw[g, half] = raw
+
+        def load_gains(lo, hi):
+            raw = keep.tile([P, (hi - lo) * GROUPS, PACK], BF16, name="gains_%d" % lo)
             nc.sync.dma_start(
                 out=raw[:],
-                in_=w_in[:, gd * KP : (gd + 1) * KP].rearrange("(p j) c -> p j c", j=PACK),
+                in_=frame_gain[lo:hi, :].rearrange("b (g p t) -> p (b g) t", p=P, t=PACK),
             )
-            w_raw[gd] = raw
+            for n in range(lo * GROUPS, hi * GROUPS):
+                gains[n] = raw[:, n - lo * GROUPS, :]
 
-        load_mel(0, 0, 2)
-        load_w(0)
-        gamma_bf = keep.tile([P, 2, PACK], BF16)
+        gamma_bf = keep.tile([P, GROUPS, PACK], BF16)
         nc.scalar.dma_start(out=gamma_bf[:], in_=gamma.rearrange("(g p t) -> p g t", p=P, t=PACK))
-        gain = keep.tile([P, B * 2, PACK], BF16)
-        nc.scalar.dma_start(
-            out=gain[:], in_=frame_gain.rearrange("b (g p t) -> p (b g) t", p=P, t=PACK)
-        )
-        shift = keep.tile([P, B * 2, PACK], BF16)
-        nc.scalar.dma_start(
-            out=shift[:], in_=offset.rearrange("b (g p t) -> p (b g) t", p=P, t=PACK)
-        )
-        load_mel(0, 1, 1)
-        v_raw = keep.tile([P, 2, PACK, S], BF16)
+        load_mel(0, 0, 2)
+        load_mel(0, 2, 4)
+        load_w(0, 0)
+        load_w(0, 1)
+        load_gains(0, 1)
+        load_mel(1, 0, 2)
+        load_mel(1, 2, 4)
+        load_w(1, 0)
+        load_w(1, 1)
+        v_raw = keep.tile([P, GROUPS, PACK, S], BF16)
         nc.sync.dma_start(
             out=v_raw[:], in_=w_bottle.rearrange("(g p j) s -> p g j s", p=P, j=PACK)
         )
-        load_w(1)
-        for b in range(1, B):
-            for fg in range(2):
-                load_mel(b, fg, 1)
+        load_mel(2, 0, PACK)
+        offsets = keep.tile([P, UNITS, PACK], BF16)
+        nc.sync.dma_start(
+            out=offsets[:], in_=offset.rearrange("b (g p t) -> p (b g) t", p=P, t=PACK)
+        )
+        load_mel(3, 0, PACK)
+        load_gains(1, B)
+        for n in range(4, B * GROUPS):
+            load_mel(n, 0, PACK)
 
-        gamma_f = keep.tile([P, 2, PACK], F32)
+        gamma_f = keep.tile([P, GROUPS, PACK], F32)
         nc.scalar.activation(out=gamma_f[:], in_=gamma_bf[:], func=ACT.Copy)
 
         def quantize(codes, scales, src):
             nc.vector.quantize_mx(out=codes.bitcast(FP8X4), scales=scales, in_=src)
 
-        def copy_on(eng, out, in_):
-            if eng == "V":
-                nc.vector.tensor_copy(out=out, in_=in_)
-            elif eng == "S":
-                nc.scalar.copy(out=out, in_=in_)
-            else:
-                nc.gpsimd.tensor_scalar(
-                    out=out, in0=in_, scalar1=1.0, scalar2=-0.0, op0=ALU.mult, op1=ALU.add
-                )
+        def multiply(out, stationary, m_cols, moving, n_cols, start, stop):
+            nc.tensor.matmul_mx(
+                out=out,
+                lhsT=stationary[0][:, m_cols].bitcast(FP8X4),
+                lhsT_scale=stationary[1][:, m_cols],
+                rhs=moving[0][:, n_cols].bitcast(FP8X4),
+                rhs_scale=moving[1][:, n_cols],
+                start=start,
+                stop=stop,
+            )
+
+        def interleave(copy, dst, src):
+            copy(
+                out=dst.rearrange("p (c i t) -> p c t i", i=RUN, t=PACK),
+                in_=src.rearrange("p t (c i) -> p c t i", i=RUN),
+            )
 
         w_codes = keep.tile([P, D], U32, align_bytes=64)
         w_scales = keep.tile([P, D], U8, align_bytes=64)
-        w_grouped = {}
+        w_grouped = keep.tile([P, GROUPS, GROUP * PACK], BF16, align_bytes=64)
 
-        def w_group(gd, eng):
-            g = keep.tile([P, KP * PACK], BF16, name="w_grouped_%d" % gd, align_bytes=64)
-            copy_on(
-                eng,
-                g[:].rearrange("p (t m j) -> p m j t", t=PACK, j=PACK),
-                w_raw[gd][:].rearrange("p j (m t) -> p m j t", t=PACK),
-            )
-            w_grouped[gd] = g
-
-        def w_quant(gd):
-            cols = slice(gd * KP, (gd + 1) * KP)
-            quantize(w_codes[:, cols], w_scales[:, cols], w_grouped[gd][:])
-
-        v_grouped = keep.tile([P, 2 * S * PACK], BF16, align_bytes=64)
-        v_codes = keep.tile([P, 2 * S], U32, align_bytes=64)
-        v_scales = keep.tile([P, 2 * S], U8, align_bytes=64)
-
-        def v_group(g, eng):
-            copy_on(
-                eng,
-                v_grouped[:, g * S * PACK : (g + 1) * S * PACK].rearrange(
-                    "p (c i j) -> p c j i", i=4, j=PACK
-                ),
-                v_raw[:, g, :, :].rearrange("p j (c i) -> p c j i", i=4),
+        def w_interleave(copy, g, half):
+            dst = w_grouped[:, g, :].rearrange("p (t m j) -> p m j t", t=PACK, j=PACK)
+            copy(
+                out=dst[:, half * P // 2 : (half + 1) * P // 2],
+                in_=w_raw[g, half][:].rearrange("p j (m t) -> p m j t", t=PACK),
             )
 
-        def v_quant():
-            for lo, hi in ((0, 512), (512, 768)):
+        def w_quantize(g, lo, hi):
+            cols = slice(g * GROUP + lo * P, g * GROUP + hi * P)
+            quantize(w_codes[:, cols], w_scales[:, cols], w_grouped[:, g, lo * GROUP : hi * GROUP])
+
+        v_grouped = keep.tile([P, GROUPS * S * PACK], BF16, align_bytes=64)
+        v_codes = keep.tile([P, GROUPS * S], U32, align_bytes=64)
+        v_scales = keep.tile([P, GROUPS * S], U8, align_bytes=64)
+
+        def v_interleave(g):
+            dst = v_grouped[:, g * S * PACK : (g + 1) * S * PACK]
+            interleave(nc.scalar.copy, dst, v_raw[:, g, :, :])
+
+        def v_quantize():
+            for lo, hi in ((0, 512), (512, GROUPS * S)):
                 quantize(v_codes[:, lo:hi], v_scales[:, lo:hi], v_grouped[:, lo * PACK : hi * PACK])
 
         x_grouped = {}
         x_quant = {}
 
-        def mel_turn(b, fg):
-            for h in range(2):
-                bank = psum.tile([P, 512], F32, tag="sbank", name="mel_bank")
-                for tt in range(2):
-                    words = mel_raw[b, fg, 2 * h + tt].bitcast(F32)
-                    for u in range(2):
-                        c = (2 * tt + u) * P
-                        nc.tensor.transpose(bank[:, c : c + P], words[:, u : 2 * P : 2], ident[:])
-                xg = work.tile([P, 2 * P * PACK], BF16, tag="xg", bufs=4, align_bytes=64)
-                nc.scalar.copy(
-                    out=xg[:].bitcast(F32).rearrange("p (t m u) -> p t m u", t=2, u=2),
-                    in_=bank[:].rearrange("p (t u m) -> p t m u", t=2, u=2),
-                )
-                x_grouped[b, fg, h] = xg
+        def mel_turn(n, half):
+            if half == 0:
+                x_grouped[n] = work.tile([P, GROUP * PACK], BF16, name="x_grouped", align_bytes=64)
+                codes = work.tile([P, GROUP], U32, name="x_codes", bufs=5, align_bytes=64)
+                scales = work.tile([P, GROUP], U8, name="x_scales", bufs=5, align_bytes=64)
+                x_quant[n] = (codes, scales)
+            bank = psum.tile([P, GROUP], F32, tag="s_ring", name="mel_bank")
+            for tt in range(2):
+                words = mel_raw[n, 2 * half + tt].bitcast(F32)
+                for u in range(2):
+                    col = (2 * tt + u) * P
+                    nc.tensor.transpose(bank[:, col : col + P], words[:, u : 2 * P : 2], ident[:])
+            dst = x_grouped[n][:, half * 2 * GROUP : (half + 1) * 2 * GROUP]
+            nc.scalar.copy(
+                out=dst.bitcast(F32).rearrange("p (t m u) -> p t m u", t=2, u=2),
+                in_=bank[:].rearrange("p (t u m) -> p t m u", t=2, u=2),
+            )
 
-        def mel_quant(b, fg):
-            codes = work.tile([P, KP], U32, tag="xq", bufs=4, align_bytes=64)
-            scales = work.tile([P, KP], U8, tag="xs", bufs=4, align_bytes=64)
-            for h in range(2):
-                cols = slice(h * 2 * P, (h + 1) * 2 * P)
-                quantize(codes[:, cols], scales[:, cols], x_grouped[b, fg, h][:])
-            x_quant[b, fg] = (codes, scales)
+        def mel_quantize(n, lo, hi):
+            codes, scales = x_quant[n]
+            cols = slice(lo * P, hi * P)
+            quantize(codes[:, cols], scales[:, cols], x_grouped[n][:, lo * GROUP : hi * GROUP])
 
         a_banks = {}
         h_bf = {}
         h_quant = {}
 
-        def stage1(s):
-            b = s // 8
-            cols = slice((s % 8) * P, (s % 8 + 1) * P)
-            for fg in range(2):
-                codes, scales = x_quant[b, fg]
-                bank = psum.tile([P, 512], F32, tag="abank", name="a_bank")
-                for t in range(PACK):
-                    fr = slice(t * P, (t + 1) * P)
-                    nc.tensor.matmul_mx(
-                        out=bank[:, fr],
-                        lhsT=codes[:, fr].bitcast(FP8X4),
-                        lhsT_scale=scales[:, fr],
-                        rhs=w_codes[:, cols].bitcast(FP8X4),
-                        rhs_scale=w_scales[:, cols],
-                        start=True,
-                        stop=True,
-                    )
-                a_banks[s, fg] = bank
-
-        def relu_gain(s):
-            b = s // 8
-            hb = work.tile([P, 2, P, PACK], BF16, tag="hb", align_bytes=64)
-            for fg in range(2):
-                nc.vector.scalar_tensor_tensor(
-                    out=hb[:, fg, :, :],
-                    in0=a_banks[s, fg][:].rearrange("p (t n) -> p n t", t=PACK),
-                    scalar=0.0,
-                    in1=gain[:, 2 * b + fg, :].unsqueeze(1).to_broadcast([P, P, PACK]),
-                    op0=ALU.max,
-                    op1=ALU.mult,
+        def stage1(s, fg):
+            b, in_b = divmod(s, GROUPS * PACK)
+            bank = psum.tile([P, GROUP], F32, tag="a_ring", name="a_bank")
+            for t in range(PACK):
+                frames = slice(t * P, (t + 1) * P)
+                features = slice(in_b * P, (in_b + 1) * P)
+                multiply(
+                    bank[:, frames], x_quant[b * GROUPS + fg], frames,
+                    (w_codes, w_scales), features, True, True,
                 )
-            h_bf[s] = hb
+            a_banks[s, fg] = bank
 
-        def h_quantize(s):
-            codes = work.tile([P, 2 * P], U32, tag="hq", align_bytes=64)
-            scales = work.tile([P, 2 * P], U8, tag="hs", align_bytes=64)
-            quantize(codes[:], scales[:], h_bf[s][:].rearrange("p g n t -> p (g n t)"))
+        def relu_gain(s, fg):
+            if s not in h_bf:
+                h_bf[s] = work.tile([P, GROUPS, P, PACK], BF16, name="h_bf", bufs=5, align_bytes=64)
+            n = s // (GROUPS * PACK) * GROUPS + fg
+            nc.vector.scalar_tensor_tensor(
+                out=h_bf[s][:, fg, :, :],
+                in0=a_banks[s, fg][:].rearrange("p (t n) -> p n t", t=PACK),
+                scalar=0.0,
+                in1=gains[n].unsqueeze(1).to_broadcast([P, P, PACK]),
+                op0=ALU.max,
+                op1=ALU.mult,
+            )
+
+        def h_quantize(s, parts=((0, GROUPS),)):
+            codes = work.tile([P, GROUPS * P], U32, name="h_codes", bufs=7, align_bytes=64)
+            scales = work.tile([P, GROUPS * P], U8, name="h_scales", bufs=7, align_bytes=64)
+            src = h_bf[s][:].rearrange("p g n t -> p (g n t)")
+            for lo, hi in parts:
+                cols = slice(lo * P, hi * P)
+                quantize(codes[:, cols], scales[:, cols], src[:, lo * GROUP : hi * GROUP])
             h_quant[s] = (codes, scales)
 
-        tanh_out = {}
         y_t = {}
 
-        def stage2(s):
-            codes, scales = h_quant[s]
-            bank = psum.tile([P, 512], F32, tag="sbank", name="z_bank")
-            for lo, hi in ((0, WIDE), (WIDE, S)):
-                for fg in range(2):
-                    ch = slice(fg * P, (fg + 1) * P)
-                    sl = slice(fg * S + lo, fg * S + hi)
-                    nc.tensor.matmul_mx(
-                        out=bank[:, lo:hi],
-                        lhsT=codes[:, ch].bitcast(FP8X4),
-                        lhsT_scale=scales[:, ch],
-                        rhs=v_codes[:, sl].bitcast(FP8X4),
-                        rhs_scale=v_scales[:, sl],
-                        start=(fg == 0),
-                        stop=(fg == 1),
+        def stage2(s, parts):
+            bank = psum.tile([P, GROUP], F32, tag="s_ring", name="z_bank")
+            base = parts[0][0]
+            width = parts[-1][1] - base
+            for lo, hi in parts:
+                for fg in range(GROUPS):
+                    multiply(
+                        bank[:, lo - base : hi - base], h_quant[s], slice(fg * P, (fg + 1) * P),
+                        (v_codes, v_scales), slice(fg * S + lo, fg * S + hi),
+                        fg == 0, fg == GROUPS - 1,
                     )
-            th = work.tile([P, S], F32, tag="th")
+            tanh = work.tile([P, width], F32, name="tanh", bufs=7)
             nc.scalar.activation(
-                out=th[:],
-                in_=bank[:, 0:S],
-                func=ACT.Tanh,
-                bias=shift[:, s // PACK, s % PACK : s % PACK + 1],
+                out=tanh[:], in_=bank[:, 0:width], func=ACT.Tanh,
+                bias=offsets[:, s // PACK, s % PACK : s % PACK + 1],
             )
-            tanh_out[s] = th
+            return tanh
 
-        def feature_gain(s, eng):
+        def y_slice(s):
             u, t = divmod(s, PACK)
-            if t == 0:
-                y_t[u] = work.tile([P, PACK, S], F32, tag="yt", name="y_t")
-            col = gamma_f[:, u % 2, t : t + 1]
-            if eng == "S":
-                nc.scalar.activation(out=y_t[u][:, t, :], in_=tanh_out[s][:], func=ACT.Copy, scale=col)
-            elif eng == "V":
-                nc.vector.tensor_scalar(
-                    out=y_t[u][:, t, :], in0=tanh_out[s][:], scalar1=col, scalar2=None, op0=ALU.mult
-                )
-            else:
-                nc.gpsimd.tensor_scalar(
-                    out=y_t[u][:, t, :], in0=tanh_out[s][:], scalar1=col, scalar2=-0.0,
-                    op0=ALU.mult, op1=ALU.add,
-                )
+            if u not in y_t:
+                y_t[u] = work.tile([P, PACK, S], F32, name="y_t")
+            return y_t[u][:, t, :], gamma_f[:, u % GROUPS, t : t + 1]
+
+        def gain_on_gpsimd(s, tanh):
+            dst, col = y_slice(s)
+            nc.gpsimd.tensor_scalar(
+                out=dst, in0=tanh[:], scalar1=col, scalar2=-0.0, op0=ALU.mult, op1=ALU.add
+            )
+
+        def gain_on_vector(s, tanh, lo, hi):
+            dst, col = y_slice(s)
+            nc.vector.tensor_scalar(
+                out=dst[:, lo:hi], in0=tanh[:], scalar1=col, scalar2=None, op0=ALU.mult
+            )
 
         def y_transpose(u, t, j, bank):
             nc.tensor.transpose(
@@ -251,122 +252,163 @@ def tile_mel_temporal_bottleneck_h3_kernel(
             )
 
         def y_rows(u):
-            b, gd = divmod(u, 2)
-            return out_0[b, :, gd * KP : (gd + 1) * KP].rearrange("(j s) d -> s j d", s=P)
+            b, g = divmod(u, GROUPS)
+            return out_0[b, :, g * GROUP : (g + 1) * GROUP].rearrange("(j s) d -> s j d", s=P)
 
-        def y_evacuate(bank, dst):
+        def y_empty(bank, dst):
             nc.scalar.copy(
                 out=dst.rearrange("s (p t) -> s p t", t=PACK),
                 in_=bank[:].rearrange("s (t p) -> s p t", t=PACK),
             )
 
         def y_store(u):
-            rows = work.tile([P, 3, KP], F32, tag="yrows", bufs=2)
-            for j in range(3):
-                bank = psum.tile([P, 512], F32, tag="sbank", name="y_bank")
+            rows = keep.tile([P, SLOT_TILES, GROUP], F32, name="y_rows_%d" % u)
+            for j in range(SLOT_TILES):
+                bank = psum.tile([P, GROUP], F32, tag="s_ring", name="y_bank")
                 for t in range(PACK):
                     y_transpose(u, t, j, bank)
-                y_evacuate(bank, rows[:, j, :])
+                y_empty(bank, rows[:, j, :])
             nc.sync.dma_start(out=y_rows(u), in_=rows[:])
 
-        y_bf = {}
-        PARTS = ((0, WIDE), (WIDE, S))
-
-        def y_round(u, part, eng):
-            lo, hi = PARTS[part]
-            yb = work.tile([P, (hi - lo) * PACK], BF16, tag="yb%d" % part, name="y_bf", bufs=2, align_bytes=64)
-            n = 1 if eng != "G" else (hi - lo) // 128
-            w = (hi - lo) // n
-            for c in range(n):
-                copy_on(
-                    eng,
-                    yb[:, c * w * PACK : (c + 1) * w * PACK].rearrange("p (c i t) -> p c t i", i=4, t=PACK),
-                    y_t[u][:, :, lo + c * w : lo + (c + 1) * w].rearrange("p t (c i) -> p c t i", i=4),
-                )
-            y_bf[u, part] = yb
-
         y_scales = keep.tile([P, B * S], U8, align_bytes=64)
+        y_bf = {}
+        y_codes = {}
 
-        def y_quant(u):
-            b, gd = divmod(u, 2)
-            codes = work.tile([P, S], U32, tag="yq", bufs=2, align_bytes=64)
-            for part in range(2):
-                lo, hi = PARTS[part]
-                quantize(
-                    codes[:, lo:hi],
-                    y_scales[4 * gd : P, b * S + lo : b * S + hi],
-                    y_bf[u, part][:],
-                )
-            dst = out_1[gd].rearrange("p m t -> p (m t)").bitcast(I32)
-            nc.sync.dma_start(out=dst[:, b * S : (b + 1) * S], in_=codes[:].bitcast(I32))
+        def y_round(copy, u, part):
+            lo, hi = part
+            tile = work.tile(
+                [P, (hi - lo) * PACK], BF16, name="y_bf_%d" % (hi - lo), align_bytes=64
+            )
+            interleave(copy, tile[:], y_t[u][:, :, lo:hi])
+            y_bf[u, part] = tile
+
+        def y_quantize(u, part):
+            b, g = divmod(u, GROUPS)
+            if u not in y_codes:
+                y_codes[u] = keep.tile([P, S], U32, name="y_codes_%d" % u, align_bytes=64)
+            lo, hi = part
+            quantize(
+                y_codes[u][:, lo:hi], y_scales[4 * g : P, b * S + lo : b * S + hi], y_bf[u, part][:]
+            )
+
+        def words_store(u):
+            b, g = divmod(u, GROUPS)
+            dst = out_1[g].rearrange("p m t -> p (m t)").bitcast(I32)
+            nc.sync.dma_start(out=dst[:, b * S : (b + 1) * S], in_=y_codes[u][:].bitcast(I32))
 
         mel_turn(0, 0)
-        w_group(0, "V")
-        w_quant(0)
-        mel_quant(0, 0)
         mel_turn(0, 1)
-        v_group(0, "V")
-        mel_quant(0, 1)
-        v_group(1, "S")
-        w_group(1, "S")
-        stage1(0)
+        mel_turn(1, 0)
+        w_interleave(nc.vector.tensor_copy, 0, 0)
+        mel_quantize(0, 0, 2)
+        w_interleave(nc.vector.tensor_copy, 0, 1)
+        mel_quantize(0, 2, 4)
+        w_quantize(0, 0, 1)
+        stage1(0, 0)
+        w_quantize(0, 1, 2)
+        stage1(1, 0)
+        w_quantize(0, 2, 4)
+        relu_gain(0, 0)
+        w_interleave(nc.scalar.copy, 1, 0)
+        mel_turn(1, 1)
+        w_interleave(nc.scalar.copy, 1, 1)
+        stage1(2, 0)
+        stage1(3, 0)
+        relu_gain(1, 0)
+        mel_quantize(1, 0, 2)
+        relu_gain(2, 0)
+        mel_quantize(1, 2, 4)
+        stage1(0, 1)
+        stage1(1, 1)
+        relu_gain(3, 0)
+        v_interleave(0)
+        v_interleave(1)
+        stage1(2, 1)
+        relu_gain(0, 1)
+        stage1(3, 1)
+        relu_gain(1, 1)
+        h_quantize(0)
+        relu_gain(2, 1)
+        w_quantize(1, 0, PACK)
+        stage1(PACK, 0)
+        stage1(PACK, 1)
+        h_quantize(1)
+        relu_gain(3, 1)
+        h_quantize(2)
+        mel_turn(2, 0)
+        mel_turn(2, 1)
+        v_quantize()
 
-        for i in range(STEPS):
-            t = i % PACK
-            if i + 1 < STEPS:
-                stage1(i + 1)
-            if i >= 2:
-                stage2(i - 2)
-            if i >= 3:
-                feature_gain(i - 3, GAMMA_ENG)
-            nxt = (i // 8 + 1, (i // 4) % 2)
-            if t == 1 and nxt[0] < B:
-                mel_turn(nxt[0], nxt[1])
-            if t == 3 and i >= 7:
-                y_store(i // PACK - 1)
-            if t == 0 and i >= 8:
-                y_round(i // PACK - 2, 1, CAST_B)
-            relu_gain(i)
-            if i >= 1:
+        end = STEPS - 1
+        done2 = 0
+        for i in range(PACK, STEPS):
+            u, t = divmod(i, PACK)
+            ahead = u + 2
+            if i < end:
+                stage1(i + 1, 0)
+                stage1(i + 1, 1)
+            upto = min(2 * (i + 1 - PACK), i - 1)
+            for s in range(done2, upto):
+                tanh = stage2(s, (WIDE, NARROW))
+                if i < end:
+                    gain_on_gpsimd(s, tanh)
+            done2 = upto
+            if t == 0 and u >= 2:
+                y_round(nc.scalar.copy, u - 2, WIDE)
+            if t == 1 and ahead < B * GROUPS:
+                mel_turn(ahead, 0)
+                mel_turn(ahead, 1)
+            if t == 2:
+                y_store(u - 1)
+            if t == 3:
+                y_round(nc.scalar.copy, u - 1, NARROW)
+            relu_gain(i, 1)
+            if i == end:
                 h_quantize(i - 1)
-            if i == 0:
-                v_quant()
-            if i == 2:
-                w_quant(1)
-            if t == 2 and nxt[0] < B:
-                mel_quant(nxt[0], nxt[1])
-            if t == 3 and 7 <= i < STEPS - 1:
-                y_round(i // PACK - 1, 0, CAST_A)
-            if t == 1 and i >= 9:
-                y_quant(i // PACK - 2)
+            relu_gain(i, 0)
+            if i < end:
+                h_quantize(i - 1)
+            if i == PACK + 1:
+                mel_quantize(2, 0, PACK)
+            if t == 1 and u >= 2:
+                y_quantize(u - 2, NARROW)
+            if t == 2 and u >= 2:
+                y_quantize(u - 2, WIDE)
+                words_store(u - 2)
+            if t == 2 and ahead < B * GROUPS:
+                mel_quantize(ahead, 0, PACK)
 
-        last = STEPS // PACK - 1
-        h_quantize(STEPS - 1)
-        feature_gain(STEPS - 3, "S")
-        stage2(STEPS - 2)
-        stage2(STEPS - 1)
-        y_round(last - 1, 0, "V")
-        y_round(last - 1, 1, "V")
-        feature_gain(STEPS - 2, "V")
-        feature_gain(STEPS - 1, "V")
+        last = UNITS - 1
+        tiles = [(j * P, (j + 1) * P) for j in range(SLOT_TILES)]
+        h_quantize(end, ((1, 2), (0, 1)))
+        gain_on_vector(end - 2, tanh, 0, S)
+        tanh = stage2(end - 1, (WIDE, NARROW))
         banks = []
-        for j in range(3):
-            bank = psum.tile([P, 512], F32, tag="abank", name="last_bank")
+        for j in range(SLOT_TILES):
+            bank = psum.tile([P, GROUP], F32, tag="a_ring", name="last_bank")
             banks.append(bank)
-        for t in range(PACK):
-            for j in range(3):
+            y_transpose(last, 0, j, bank)
+        tanh_tiles = [stage2(end, (part,)) for part in tiles]
+        y_round(nc.vector.tensor_copy, last - 1, WIDE)
+        gain_on_vector(end - 1, tanh, 0, S)
+        for t in (1, 2):
+            for j in range(SLOT_TILES):
                 y_transpose(last, t, j, banks[j])
-        y_quant(last - 1)
-        y_round(last, 0, "V")
-        y_round(last, 1, "V")
-        for j in range(2):
-            rows = keep.tile([P, KP], F32, name="last_rows_%d" % j)
-            y_evacuate(banks[j], rows[:])
-            nc.sync.dma_start(out=y_rows(last)[:, j, :], in_=rows[:])
-        rows = keep.tile([P, KP], F32, name="last_rows_2")
-        y_evacuate(banks[2], rows[:])
-        nc.scalar.dma_start(out=y_rows(last)[:, 2, :], in_=rows[:])
-        y_quant(last)
+        for j, part in enumerate(tiles):
+            gain_on_vector(end, tanh_tiles[j], part[0], part[1])
+            y_transpose(last, PACK - 1, j, banks[j])
+            rows = keep.tile([P, GROUP], F32, name="last_rows_%d" % j)
+            y_empty(banks[j], rows[:])
+            queue = nc.scalar if j == SLOT_TILES - 1 else nc.sync
+            queue.dma_start(out=y_rows(last)[:, j, :], in_=rows[:])
+            if j < 2:
+                y_quantize(last - 1, (NARROW, WIDE)[j])
+        words_store(last - 1)
+        for part in (WIDE, NARROW):
+            y_round(nc.vector.tensor_copy, last, part)
+        for part in (WIDE, NARROW):
+            y_quantize(last, part)
+        words_store(last)
         for q in range(4):
             nc.sync.dma_start(
                 out=out_2[:, 4 * q : 4 * q + 4, :].bitcast(I32),

from contextlib import ExitStack

import concourse.mybir as mybir
from concourse.masks import make_identity

B, T, F, D, S = 4, 1024, 512, 1024, 384
FLOPS = 2 * B * T * F * D + 2 * B * S * T * D

F32 = mybir.dt.float32
BF16 = mybir.dt.bfloat16
I32 = mybir.dt.int32
U32 = mybir.dt.uint32
U8 = mybir.dt.uint8
FP8X4 = mybir.dt.float8_e4m3fn_x4
ACT = mybir.ActivationFunctionType
ALU = mybir.AluOpType

P = 128
PACK = 4
GROUP = P * PACK
GROUPS = 2
UNITS = B * GROUPS
STEPS = UNITS * PACK
SLOT_TILES = S // P
RUN = 4
WIDE = (0, 256)
NARROW = (256, S)


def tile_mel_temporal_bottleneck_h3_kernel(
    tc, mel, w_in, frame_gain, w_bottle, offset, gamma, out_0, out_1, out_2
):
    nc = tc.nc
    with ExitStack() as ctx:
        keep = ctx.enter_context(tc.tile_pool(name="keep", bufs=1))
        work = ctx.enter_context(tc.tile_pool(name="work", bufs=4))
        psum = ctx.enter_context(tc.psum_pool(name="psum", bufs=4))
        ctx.enter_context(tc.manual_schedule())

        ident = keep.tile([P, P], F32)
        make_identity(nc, ident[:])

        mel_raw = {}
        w_raw = {}
        gains = {}

        def load_mel(n, lo, hi):
            first = (n % GROUPS) * GROUP
            rows = mel[n // GROUPS, first : first + GROUP, :].rearrange("(m t) k -> m t k", t=PACK)
            raw = keep.tile([P, hi - lo, F], BF16, name="mel_%d_%d" % (n, lo))
            nc.sync.dma_start(out=raw[:], in_=rows[:, lo:hi, :])
            for t in range(lo, hi):
                mel_raw[n, t] = raw[:, t - lo, :]

        def load_w(g, half):
            raw = keep.tile([P, PACK, GROUP // 2], BF16, name="w_raw_%d_%d" % (g, half))
            lo = g * GROUP + half * GROUP // 2
            nc.sync.dma_start(
                out=raw[:], in_=w_in[:, lo : lo + GROUP // 2].rearrange("(p j) c -> p j c", j=PACK)
            )
            w_raw[g, half] = raw

        def load_gains(lo, hi):
            raw = keep.tile([P, (hi - lo) * GROUPS, PACK], BF16, name="gains_%d" % lo)
            nc.sync.dma_start(
                out=raw[:],
                in_=frame_gain[lo:hi, :].rearrange("b (g p t) -> p (b g) t", p=P, t=PACK),
            )
            for n in range(lo * GROUPS, hi * GROUPS):
                gains[n] = raw[:, n - lo * GROUPS, :]

        gamma_bf = keep.tile([P, GROUPS, PACK], BF16)
        nc.scalar.dma_start(out=gamma_bf[:], in_=gamma.rearrange("(g p t) -> p g t", p=P, t=PACK))
        load_mel(0, 0, 2)
        load_mel(0, 2, 4)
        load_w(0, 0)
        load_w(0, 1)
        load_gains(0, 1)
        load_mel(1, 0, 2)
        load_mel(1, 2, 4)
        load_w(1, 0)
        load_w(1, 1)
        v_raw = keep.tile([P, GROUPS, PACK, S], BF16)
        nc.sync.dma_start(
            out=v_raw[:], in_=w_bottle.rearrange("(g p j) s -> p g j s", p=P, j=PACK)
        )
        load_mel(2, 0, PACK)
        offsets = keep.tile([P, UNITS, PACK], BF16)
        nc.sync.dma_start(
            out=offsets[:], in_=offset.rearrange("b (g p t) -> p (b g) t", p=P, t=PACK)
        )
        load_mel(3, 0, PACK)
        load_gains(1, B)
        for n in range(4, B * GROUPS):
            load_mel(n, 0, PACK)

        gamma_f = keep.tile([P, GROUPS, PACK], F32)
        nc.scalar.activation(out=gamma_f[:], in_=gamma_bf[:], func=ACT.Copy)

        def quantize(codes, scales, src):
            nc.vector.quantize_mx(out=codes.bitcast(FP8X4), scales=scales, in_=src)

        def multiply(out, stationary, m_cols, moving, n_cols, start, stop):
            nc.tensor.matmul_mx(
                out=out,
                lhsT=stationary[0][:, m_cols].bitcast(FP8X4),
                lhsT_scale=stationary[1][:, m_cols],
                rhs=moving[0][:, n_cols].bitcast(FP8X4),
                rhs_scale=moving[1][:, n_cols],
                start=start,
                stop=stop,
            )

        def interleave(copy, dst, src):
            copy(
                out=dst.rearrange("p (c i t) -> p c t i", i=RUN, t=PACK),
                in_=src.rearrange("p t (c i) -> p c t i", i=RUN),
            )

        w_codes = keep.tile([P, D], U32, align_bytes=64)
        w_scales = keep.tile([P, D], U8, align_bytes=64)
        w_grouped = keep.tile([P, GROUPS, GROUP * PACK], BF16, align_bytes=64)

        def w_interleave(copy, g, half):
            dst = w_grouped[:, g, :].rearrange("p (t m j) -> p m j t", t=PACK, j=PACK)
            copy(
                out=dst[:, half * P // 2 : (half + 1) * P // 2],
                in_=w_raw[g, half][:].rearrange("p j (m t) -> p m j t", t=PACK),
            )

        def w_quantize(g, lo, hi):
            cols = slice(g * GROUP + lo * P, g * GROUP + hi * P)
            quantize(w_codes[:, cols], w_scales[:, cols], w_grouped[:, g, lo * GROUP : hi * GROUP])

        v_grouped = keep.tile([P, GROUPS * S * PACK], BF16, align_bytes=64)
        v_codes = keep.tile([P, GROUPS * S], U32, align_bytes=64)
        v_scales = keep.tile([P, GROUPS * S], U8, align_bytes=64)

        def v_interleave(g):
            dst = v_grouped[:, g * S * PACK : (g + 1) * S * PACK]
            interleave(nc.scalar.copy, dst, v_raw[:, g, :, :])

        def v_quantize():
            for lo, hi in ((0, 512), (512, GROUPS * S)):
                quantize(v_codes[:, lo:hi], v_scales[:, lo:hi], v_grouped[:, lo * PACK : hi * PACK])

        x_grouped = {}
        x_quant = {}

        def mel_turn(n, half):
            if half == 0:
                x_grouped[n] = work.tile([P, GROUP * PACK], BF16, name="x_grouped", align_bytes=64)
                codes = work.tile([P, GROUP], U32, name="x_codes", bufs=5, align_bytes=64)
                scales = work.tile([P, GROUP], U8, name="x_scales", bufs=5, align_bytes=64)
                x_quant[n] = (codes, scales)
            bank = psum.tile([P, GROUP], F32, tag="s_ring", name="mel_bank")
            for tt in range(2):
                words = mel_raw[n, 2 * half + tt].bitcast(F32)
                for u in range(2):
                    col = (2 * tt + u) * P
                    nc.tensor.transpose(bank[:, col : col + P], words[:, u : 2 * P : 2], ident[:])
            dst = x_grouped[n][:, half * 2 * GROUP : (half + 1) * 2 * GROUP]
            nc.scalar.copy(
                out=dst.bitcast(F32).rearrange("p (t m u) -> p t m u", t=2, u=2),
                in_=bank[:].rearrange("p (t u m) -> p t m u", t=2, u=2),
            )

        def mel_quantize(n, lo, hi):
            codes, scales = x_quant[n]
            cols = slice(lo * P, hi * P)
            quantize(codes[:, cols], scales[:, cols], x_grouped[n][:, lo * GROUP : hi * GROUP])

        a_banks = {}
        h_bf = {}
        h_quant = {}

        def stage1(s, fg):
            b, in_b = divmod(s, GROUPS * PACK)
            bank = psum.tile([P, GROUP], F32, tag="a_ring", name="a_bank")
            for t in range(PACK):
                frames = slice(t * P, (t + 1) * P)
                features = slice(in_b * P, (in_b + 1) * P)
                multiply(
                    bank[:, frames], x_quant[b * GROUPS + fg], frames,
                    (w_codes, w_scales), features, True, True,
                )
            a_banks[s, fg] = bank

        def relu_gain(s, fg):
            if s not in h_bf:
                h_bf[s] = work.tile([P, GROUPS, P, PACK], BF16, name="h_bf", bufs=5, align_bytes=64)
            n = s // (GROUPS * PACK) * GROUPS + fg
            nc.vector.scalar_tensor_tensor(
                out=h_bf[s][:, fg, :, :],
                in0=a_banks[s, fg][:].rearrange("p (t n) -> p n t", t=PACK),
                scalar=0.0,
                in1=gains[n].unsqueeze(1).to_broadcast([P, P, PACK]),
                op0=ALU.max,
                op1=ALU.mult,
            )

        def h_quantize(s, parts=((0, GROUPS),)):
            codes = work.tile([P, GROUPS * P], U32, name="h_codes", bufs=7, align_bytes=64)
            scales = work.tile([P, GROUPS * P], U8, name="h_scales", bufs=7, align_bytes=64)
            src = h_bf[s][:].rearrange("p g n t -> p (g n t)")
            for lo, hi in parts:
                cols = slice(lo * P, hi * P)
                quantize(codes[:, cols], scales[:, cols], src[:, lo * GROUP : hi * GROUP])
            h_quant[s] = (codes, scales)

        y_t = {}

        def stage2(s, parts):
            bank = psum.tile([P, GROUP], F32, tag="s_ring", name="z_bank")
            base = parts[0][0]
            width = parts[-1][1] - base
            for lo, hi in parts:
                for fg in range(GROUPS):
                    multiply(
                        bank[:, lo - base : hi - base], h_quant[s], slice(fg * P, (fg + 1) * P),
                        (v_codes, v_scales), slice(fg * S + lo, fg * S + hi),
                        fg == 0, fg == GROUPS - 1,
                    )
            tanh = work.tile([P, width], F32, name="tanh", bufs=7)
            nc.scalar.activation(
                out=tanh[:], in_=bank[:, 0:width], func=ACT.Tanh,
                bias=offsets[:, s // PACK, s % PACK : s % PACK + 1],
            )
            return tanh

        def y_slice(s):
            u, t = divmod(s, PACK)
            if u not in y_t:
                y_t[u] = work.tile([P, PACK, S], F32, name="y_t")
            return y_t[u][:, t, :], gamma_f[:, u % GROUPS, t : t + 1]

        def gain_on_gpsimd(s, tanh):
            dst, col = y_slice(s)
            nc.gpsimd.tensor_scalar(
                out=dst, in0=tanh[:], scalar1=col, scalar2=-0.0, op0=ALU.mult, op1=ALU.add
            )

        def gain_on_vector(s, tanh, lo, hi):
            dst, col = y_slice(s)
            nc.vector.tensor_scalar(
                out=dst[:, lo:hi], in0=tanh[:], scalar1=col, scalar2=None, op0=ALU.mult
            )

        def y_transpose(u, t, j, bank):
            nc.tensor.transpose(
                bank[:, t * P : (t + 1) * P], y_t[u][:, t, j * P : (j + 1) * P], ident[:]
            )

        def y_rows(u):
            b, g = divmod(u, GROUPS)
            return out_0[b, :, g * GROUP : (g + 1) * GROUP].rearrange("(j s) d -> s j d", s=P)

        def y_empty(bank, dst):
            nc.scalar.copy(
                out=dst.rearrange("s (p t) -> s p t", t=PACK),
                in_=bank[:].rearrange("s (t p) -> s p t", t=PACK),
            )

        def y_store(u):
            rows = keep.tile([P, SLOT_TILES, GROUP], F32, name="y_rows_%d" % u)
            for j in range(SLOT_TILES):
                bank = psum.tile([P, GROUP], F32, tag="s_ring", name="y_bank")
                for t in range(PACK):
                    y_transpose(u, t, j, bank)
                y_empty(bank, rows[:, j, :])
            nc.sync.dma_start(out=y_rows(u), in_=rows[:])

        y_scales = keep.tile([P, B * S], U8, align_bytes=64)
        y_bf = {}
        y_codes = {}

        def y_round(copy, u, part):
            lo, hi = part
            tile = work.tile(
                [P, (hi - lo) * PACK], BF16, name="y_bf_%d" % (hi - lo), align_bytes=64
            )
            interleave(copy, tile[:], y_t[u][:, :, lo:hi])
            y_bf[u, part] = tile

        def y_quantize(u, part):
            b, g = divmod(u, GROUPS)
            if u not in y_codes:
                y_codes[u] = keep.tile([P, S], U32, name="y_codes_%d" % u, align_bytes=64)
            lo, hi = part
            quantize(
                y_codes[u][:, lo:hi], y_scales[4 * g : P, b * S + lo : b * S + hi], y_bf[u, part][:]
            )

        def words_store(u):
            b, g = divmod(u, GROUPS)
            dst = out_1[g].rearrange("p m t -> p (m t)").bitcast(I32)
            nc.sync.dma_start(out=dst[:, b * S : (b + 1) * S], in_=y_codes[u][:].bitcast(I32))

        mel_turn(0, 0)
        mel_turn(0, 1)
        mel_turn(1, 0)
        w_interleave(nc.vector.tensor_copy, 0, 0)
        mel_quantize(0, 0, 2)
        w_interleave(nc.vector.tensor_copy, 0, 1)
        mel_quantize(0, 2, 4)
        w_quantize(0, 0, 1)
        stage1(0, 0)
        w_quantize(0, 1, 2)
        stage1(1, 0)
        w_quantize(0, 2, 4)
        relu_gain(0, 0)
        w_interleave(nc.scalar.copy, 1, 0)
        mel_turn(1, 1)
        w_interleave(nc.scalar.copy, 1, 1)
        stage1(2, 0)
        stage1(3, 0)
        relu_gain(1, 0)
        mel_quantize(1, 0, 2)
        relu_gain(2, 0)
        mel_quantize(1, 2, 4)
        stage1(0, 1)
        stage1(1, 1)
        relu_gain(3, 0)
        v_interleave(0)
        v_interleave(1)
        stage1(2, 1)
        relu_gain(0, 1)
        stage1(3, 1)
        relu_gain(1, 1)
        h_quantize(0)
        relu_gain(2, 1)
        w_quantize(1, 0, PACK)
        stage1(PACK, 0)
        stage1(PACK, 1)
        h_quantize(1)
        relu_gain(3, 1)
        h_quantize(2)
        mel_turn(2, 0)
        mel_turn(2, 1)
        v_quantize()

        end = STEPS - 1
        done2 = 0
        for i in range(PACK, STEPS):
            u, t = divmod(i, PACK)
            ahead = u + 2
            if i < end:
                stage1(i + 1, 0)
                stage1(i + 1, 1)
            upto = min(2 * (i + 1 - PACK), i - 1)
            for s in range(done2, upto):
                tanh = stage2(s, (WIDE, NARROW))
                if i < end:
                    gain_on_gpsimd(s, tanh)
            done2 = upto
            if t == 0 and u >= 2:
                y_round(nc.scalar.copy, u - 2, WIDE)
            if t == 1 and ahead < B * GROUPS:
                mel_turn(ahead, 0)
                mel_turn(ahead, 1)
            if t == 2:
                y_store(u - 1)
            if t == 3:
                y_round(nc.scalar.copy, u - 1, NARROW)
            relu_gain(i, 1)
            if i == end:
                h_quantize(i - 1)
            relu_gain(i, 0)
            if i < end:
                h_quantize(i - 1)
            if i == PACK + 1:
                mel_quantize(2, 0, PACK)
            if t == 1 and u >= 2:
                y_quantize(u - 2, NARROW)
            if t == 2 and u >= 2:
                y_quantize(u - 2, WIDE)
                words_store(u - 2)
            if t == 2 and ahead < B * GROUPS:
                mel_quantize(ahead, 0, PACK)

        last = UNITS - 1
        tiles = [(j * P, (j + 1) * P) for j in range(SLOT_TILES)]
        h_quantize(end, ((1, 2), (0, 1)))
        gain_on_vector(end - 2, tanh, 0, S)
        tanh = stage2(end - 1, (WIDE, NARROW))
        banks = []
        for j in range(SLOT_TILES):
            bank = psum.tile([P, GROUP], F32, tag="a_ring", name="last_bank")
            banks.append(bank)
            y_transpose(last, 0, j, bank)
        tanh_tiles = [stage2(end, (part,)) for part in tiles]
        y_round(nc.vector.tensor_copy, last - 1, WIDE)
        gain_on_vector(end - 1, tanh, 0, S)
        for t in (1, 2):
            for j in range(SLOT_TILES):
                y_transpose(last, t, j, banks[j])
        for j, part in enumerate(tiles):
            gain_on_vector(end, tanh_tiles[j], part[0], part[1])
            y_transpose(last, PACK - 1, j, banks[j])
            rows = keep.tile([P, GROUP], F32, name="last_rows_%d" % j)
            y_empty(banks[j], rows[:])
            queue = nc.scalar if j == SLOT_TILES - 1 else nc.sync
            queue.dma_start(out=y_rows(last)[:, j, :], in_=rows[:])
            if j < 2:
                y_quantize(last - 1, (NARROW, WIDE)[j])
        words_store(last - 1)
        for part in (WIDE, NARROW):
            y_round(nc.vector.tensor_copy, last, part)
        for part in (WIDE, NARROW):
            y_quantize(last, part)
        words_store(last)
        for q in range(4):
            nc.sync.dma_start(
                out=out_2[:, 4 * q : 4 * q + 4, :].bitcast(I32),
                in_=y_scales[32 * q : 32 * q + 8, :].bitcast(I32),
            )
